import numpy as np
import ml_dtypes

BF16 = ml_dtypes.bfloat16


def bf(x):
    return np.asarray(x, np.float32).astype(BF16)


def f32(x):
    return np.asarray(x, np.float32)


def f64(x):
    return np.asarray(x).astype(np.float64)


def striped(idx):
    return np.tile(idx.reshape(-1, 16).T, (8, 1))


S, K, M, N = 4096, 128, 256, 768


def setup_inputs():
    return {"table": bf(np.random.standard_normal((S, K))), "w": bf(np.random.standard_normal((K, M)) / np.sqrt(K)), "s": f32(0.5 + np.random.random_sample((M, 1))), "b": f32(0.5 * np.random.standard_normal((M, 1))), "offs": striped(np.random.permutation(np.tile(np.arange(S), 2))[:N])}


def reference(table, w, s, b, offs):
    idx = offs[:16].T.reshape(-1)
    x = f64(table)[idx].T
    y = f64(w).T @ x
    return y * f64(s) + f64(b)

@@ -1,0 +1,76 @@
+import concourse.mybir as mybir
+from concourse.masks import make_identity
+
+BF16, F32, U16 = mybir.dt.bfloat16, mybir.dt.float32, mybir.dt.uint16
+MULT, ADD = mybir.AluOpType.mult, mybir.AluOpType.add
+IDENTITY = mybir.ActivationFunctionType.Identity
+
+P = 128
+WORDS, K, M, N = 4096, 128, 256, 768
+FLOPS = 2 * K * M * N
+
+GROUP_BLOCKS = 4
+GROUP_WORDS = GROUP_BLOCKS * P
+GROUPS = WORDS // GROUP_WORDS
+PIECE = 384
+PIECES = N // PIECE
+M_BLOCKS = M // P
+
+
+def tile_gather_matmul_kernel(tc, table, w, s, b, offs, out):
+    nc = tc.nc
+    with (
+        tc.tile_pool(name="held", bufs=1) as held,
+        tc.psum_pool(name="flip_psum", bufs=4) as flip_psum,
+        tc.psum_pool(name="prod_psum", bufs=1) as prod_psum,
+    ):
+        offsets = held.tile([P, N // 16], U16, name="offsets")
+        nc.sync.dma_start(offsets[:], offs)
+
+        identity = held.tile([P, P], BF16, name="identity")
+        make_identity(nc, identity[:])
+
+        rows = [held.tile([P, GROUP_BLOCKS, K], BF16, name=f"rows{g}") for g in range(GROUPS)]
+        for g in range(GROUPS):
+            queue = nc.sync if g % 2 == 0 else nc.scalar
+            queue.dma_start(
+                rows[g][:],
+                table[g * GROUP_WORDS : (g + 1) * GROUP_WORDS, :].rearrange("(a p) k -> p a k", p=P),
+            )
+
+        weights = held.tile([K, M], BF16, name="weights")
+        nc.gpsimd.dma_start(weights[:], w)
+        gain = held.tile([P, M_BLOCKS], F32, name="gain")
+        shift = held.tile([P, M_BLOCKS], F32, name="shift")
+        with nc.allow_non_contiguous_dma(reason="one float32 value to a partition"):
+            nc.gpsimd.dma_start(gain[:], s.rearrange("(a p) o -> p (a o)", p=P))
+            nc.gpsimd.dma_start(shift[:], b.rearrange("(a p) o -> p (a o)", p=P))
+
+        flipped = held.tile([K, WORDS], BF16, name="flipped")
+        for g in range(GROUPS):
+            bank = flip_psum.tile([K, GROUP_WORDS], BF16, name="bank")
+            for a in range(GROUP_BLOCKS):
+                nc.tensor.transpose(bank[:, a * P : (a + 1) * P], rows[g][:, a, :], identity[:])
+            window_part = flipped[:, g * GROUP_WORDS : (g + 1) * GROUP_WORDS]
+            if g % 2 == 0:
+                nc.vector.tensor_copy(window_part, bank[:])
+            else:
+                nc.scalar.copy(window_part, bank[:])
+
+        for piece in range(PIECES):
+            picked = flipped[:].indirect(offsets[:, piece * (PIECE // 16) : (piece + 1) * (PIECE // 16)])
+            for mb in range(M_BLOCKS):
+                product = prod_psum.tile([P, PIECE], F32, name=f"product{piece}_{mb}")
+                nc.tensor.matmul(product[:], weights[:, mb * P : (mb + 1) * P], picked, start=True, stop=True)
+                result = held.tile([P, PIECE], F32, name=f"result{piece}_{mb}")
+                out_part = out[mb * P : (mb + 1) * P, piece * PIECE : (piece + 1) * PIECE]
+                if mb == 0:
+                    nc.vector.tensor_scalar(
+                        result[:], product[:], gain[:, mb : mb + 1], shift[:, mb : mb + 1], MULT, ADD
+                    )
+                    nc.sync.dma_start(out_part, result[:])
+                else:
+                    nc.scalar.activation(
+                        result[:], product[:], IDENTITY, bias=shift[:, mb : mb + 1], scale=gain[:, mb : mb + 1]
+                    )
+                    nc.scalar.dma_start(out_part, result[:])

@@ -12,7 +12,8 @@ FLOPS = 2 * K * M * N
 GROUP_BLOCKS = 4
 GROUP_WORDS = GROUP_BLOCKS * P
 GROUPS = WORDS // GROUP_WORDS
-PIECE = 384
+WARM_FIRST = 3
+PIECE = 256
 PIECES = N // PIECE
 M_BLOCKS = M // P
 
@@ -21,46 +22,54 @@ def tile_gather_matmul_kernel(tc, table, w, s, b, offs, out):
     nc = tc.nc
     with (
         tc.tile_pool(name="held", bufs=1) as held,
-        tc.psum_pool(name="flip_psum", bufs=4) as flip_psum,
-        tc.psum_pool(name="prod_psum", bufs=1) as prod_psum,
+        tc.psum_pool(name="unread_psum", bufs=1) as unread_psum,
+        tc.psum_pool(name="banks", bufs=7) as banks,
     ):
+        rows = [held.tile([P, GROUP_BLOCKS, K], BF16, name=f"rows{g}") for g in range(GROUPS)]
+        for g in range(GROUPS):
+            first = g * GROUP_WORDS
+            nc.sync.dma_start(rows[g][:], table[first : first + GROUP_WORDS, :].rearrange("(p a) k -> p a k", p=P))
+
         offsets = held.tile([P, N // 16], U16, name="offsets")
         nc.sync.dma_start(offsets[:], offs)
+        weights = held.tile([K, M], BF16, name="weights")
+        nc.scalar.dma_start(weights[:], w)
+
+        zeros = held.tile([P, GROUP_WORDS], BF16, name="zeros")
+        nc.vector.memset(zeros[:], 0.0)
+        unread = unread_psum.tile([P, GROUP_WORDS], F32, name="unread")
+        for repeat in range(WARM_FIRST):
+            nc.tensor.matmul(unread[:], zeros[:, 0:P], zeros[:], start=True, stop=True)
 
         identity = held.tile([P, P], BF16, name="identity")
         make_identity(nc, identity[:])
 
-        rows = [held.tile([P, GROUP_BLOCKS, K], BF16, name=f"rows{g}") for g in range(GROUPS)]
-        for g in range(GROUPS):
-            queue = nc.sync if g % 2 == 0 else nc.scalar
-            queue.dma_start(
-                rows[g][:],
-                table[g * GROUP_WORDS : (g + 1) * GROUP_WORDS, :].rearrange("(a p) k -> p a k", p=P),
-            )
+        dummy = held.tile([P, 1], F32, name="dummy")
+        nc.scalar.activation(dummy[:], zeros[:, 0:1], IDENTITY)
 
-        weights = held.tile([K, M], BF16, name="weights")
-        nc.gpsimd.dma_start(weights[:], w)
         gain = held.tile([P, M_BLOCKS], F32, name="gain")
         shift = held.tile([P, M_BLOCKS], F32, name="shift")
-        with nc.allow_non_contiguous_dma(reason="one float32 value to a partition"):
-            nc.gpsimd.dma_start(gain[:], s.rearrange("(a p) o -> p (a o)", p=P))
-            nc.gpsimd.dma_start(shift[:], b.rearrange("(a p) o -> p (a o)", p=P))
+        nc.gpsimd.dma_start(gain[:], s.rearrange("(a p) o -> p (a o)", p=P))
+        nc.gpsimd.dma_start(shift[:], b.rearrange("(a p) o -> p (a o)", p=P))
 
         flipped = held.tile([K, WORDS], BF16, name="flipped")
         for g in range(GROUPS):
-            bank = flip_psum.tile([K, GROUP_WORDS], BF16, name="bank")
+            bank = banks.tile([K, GROUP_WORDS], BF16, name="bank")
             for a in range(GROUP_BLOCKS):
                 nc.tensor.transpose(bank[:, a * P : (a + 1) * P], rows[g][:, a, :], identity[:])
-            window_part = flipped[:, g * GROUP_WORDS : (g + 1) * GROUP_WORDS]
+            if g % 2 == 1 and g < GROUPS - 1:
+                nc.tensor.matmul(unread[:], identity[:], rows[g][:].rearrange("p a k -> p (a k)"), start=True, stop=True)
+            window_part = flipped[:, g * GROUP_WORDS : (g + 1) * GROUP_WORDS].rearrange("k (p a) -> k p a", p=P)
+            in_word_order = bank[:].rearrange("k (a p) -> k p a", p=P)
             if g % 2 == 0:
-                nc.vector.tensor_copy(window_part, bank[:])
+                nc.vector.tensor_copy(window_part, in_word_order)
             else:
-                nc.scalar.copy(window_part, bank[:])
+                nc.scalar.copy(window_part, in_word_order)
 
         for piece in range(PIECES):
             picked = flipped[:].indirect(offsets[:, piece * (PIECE // 16) : (piece + 1) * (PIECE // 16)])
             for mb in range(M_BLOCKS):
-                product = prod_psum.tile([P, PIECE], F32, name=f"product{piece}_{mb}")
+                product = banks.tile([P, PIECE], F32, name="product", tag="bank")
                 nc.tensor.matmul(product[:], weights[:, mb * P : (mb + 1) * P], picked, start=True, stop=True)
                 result = held.tile([P, PIECE], F32, name=f"result{piece}_{mb}")
                 out_part = out[mb * P : (mb + 1) * P, piece * PIECE : (piece + 1) * PIECE]
@@ -68,9 +77,8 @@ def tile_gather_matmul_kernel(tc, table, w, s, b, offs, out):
                     nc.vector.tensor_scalar(
                         result[:], product[:], gain[:, mb : mb + 1], shift[:, mb : mb + 1], MULT, ADD
                     )
-                    nc.sync.dma_start(out_part, result[:])
                 else:
                     nc.scalar.activation(
                         result[:], product[:], IDENTITY, bias=shift[:, mb : mb + 1], scale=gain[:, mb : mb + 1]
                     )
-                    nc.scalar.dma_start(out_part, result[:])
+                nc.sync.dma_start(out_part, result[:])

import concourse.mybir as mybir
from concourse.masks import make_identity

BF16, F32, U16 = mybir.dt.bfloat16, mybir.dt.float32, mybir.dt.uint16
MULT, ADD = mybir.AluOpType.mult, mybir.AluOpType.add
IDENTITY = mybir.ActivationFunctionType.Identity

P = 128
WORDS, K, M, N = 4096, 128, 256, 768
FLOPS = 2 * K * M * N

GROUP_BLOCKS = 4
GROUP_WORDS = GROUP_BLOCKS * P
GROUPS = WORDS // GROUP_WORDS
WARM_FIRST = 3
PIECE = 256
PIECES = N // PIECE
M_BLOCKS = M // P


def tile_gather_matmul_kernel(tc, table, w, s, b, offs, out):
    nc = tc.nc
    with (
        tc.tile_pool(name="held", bufs=1) as held,
        tc.psum_pool(name="unread_psum", bufs=1) as unread_psum,
        tc.psum_pool(name="banks", bufs=7) as banks,
    ):
        rows = [held.tile([P, GROUP_BLOCKS, K], BF16, name=f"rows{g}") for g in range(GROUPS)]
        for g in range(GROUPS):
            first = g * GROUP_WORDS
            nc.sync.dma_start(rows[g][:], table[first : first + GROUP_WORDS, :].rearrange("(p a) k -> p a k", p=P))

        offsets = held.tile([P, N // 16], U16, name="offsets")
        nc.sync.dma_start(offsets[:], offs)
        weights = held.tile([K, M], BF16, name="weights")
        nc.scalar.dma_start(weights[:], w)

        zeros = held.tile([P, GROUP_WORDS], BF16, name="zeros")
        nc.vector.memset(zeros[:], 0.0)
        unread = unread_psum.tile([P, GROUP_WORDS], F32, name="unread")
        for repeat in range(WARM_FIRST):
            nc.tensor.matmul(unread[:], zeros[:, 0:P], zeros[:], start=True, stop=True)

        identity = held.tile([P, P], BF16, name="identity")
        make_identity(nc, identity[:])

        dummy = held.tile([P, 1], F32, name="dummy")
        nc.scalar.activation(dummy[:], zeros[:, 0:1], IDENTITY)

        gain = held.tile([P, M_BLOCKS], F32, name="gain")
        shift = held.tile([P, M_BLOCKS], F32, name="shift")
        nc.gpsimd.dma_start(gain[:], s.rearrange("(a p) o -> p (a o)", p=P))
        nc.gpsimd.dma_start(shift[:], b.rearrange("(a p) o -> p (a o)", p=P))

        flipped = held.tile([K, WORDS], BF16, name="flipped")
        for g in range(GROUPS):
            bank = banks.tile([K, GROUP_WORDS], BF16, name="bank")
            for a in range(GROUP_BLOCKS):
                nc.tensor.transpose(bank[:, a * P : (a + 1) * P], rows[g][:, a, :], identity[:])
            if g % 2 == 1 and g < GROUPS - 1:
                nc.tensor.matmul(unread[:], identity[:], rows[g][:].rearrange("p a k -> p (a k)"), start=True, stop=True)
            window_part = flipped[:, g * GROUP_WORDS : (g + 1) * GROUP_WORDS].rearrange("k (p a) -> k p a", p=P)
            in_word_order = bank[:].rearrange("k (a p) -> k p a", p=P)
            if g % 2 == 0:
                nc.vector.tensor_copy(window_part, in_word_order)
            else:
                nc.scalar.copy(window_part, in_word_order)

        for piece in range(PIECES):
            picked = flipped[:].indirect(offsets[:, piece * (PIECE // 16) : (piece + 1) * (PIECE // 16)])
            for mb in range(M_BLOCKS):
                product = banks.tile([P, PIECE], F32, name="product", tag="bank")
                nc.tensor.matmul(product[:], weights[:, mb * P : (mb + 1) * P], picked, start=True, stop=True)
                result = held.tile([P, PIECE], F32, name=f"result{piece}_{mb}")
                out_part = out[mb * P : (mb + 1) * P, piece * PIECE : (piece + 1) * PIECE]
                if mb == 0:
                    nc.vector.tensor_scalar(
                        result[:], product[:], gain[:, mb : mb + 1], shift[:, mb : mb + 1], MULT, ADD
                    )
                else:
                    nc.scalar.activation(
                        result[:], product[:], IDENTITY, bias=shift[:, mb : mb + 1], scale=gain[:, mb : mb + 1]
                    )
                nc.sync.dma_start(out_part, result[:])
